import numpy as np
import ml_dtypes


def mxq(x, axis, fmt="e4m3"):
    dtype, down = {"e4m3": (ml_dtypes.float8_e4m3fn, 7), "e5m2": (ml_dtypes.float8_e5m2, 14)}[fmt]
    v = np.moveaxis(np.asarray(x, np.float32).astype(ml_dtypes.bfloat16).astype(np.float64), axis, -1)
    blocks = v.reshape(v.shape[:-1] + (-1, 32))
    amax = np.abs(blocks).max(-1, keepdims=True)
    byte = np.maximum(np.where(amax > 0, np.frexp(amax)[1] - 1 + 127, 0) - down, 1)
    scale = np.exp2(byte - 127.0)
    codes = (blocks / scale).astype(np.float32).astype(dtype).astype(np.float64)
    return np.moveaxis((codes * scale).reshape(v.shape), -1, axis)


WIDE = False


def mx_kscale(k):
    if not WIDE:
        return np.ones(k)
    levels = np.array([30, -30])
    if k % 512:
        return np.exp2(np.random.permutation(np.resize(levels, k // 32))).repeat(32)
    a = np.empty((k // 512, 16))
    for p in range(k // 512):
        a[p, :8] = np.random.permutation(np.resize(levels, 8))
        for g in range(8):
            far = levels[np.abs(levels - a[p, g]) >= 10]
            a[p, g + 8] = far[np.random.randint(len(far))]
    return np.exp2(a.ravel()).repeat(32)


def f64(x):
    return np.asarray(x).astype(np.float64)


def striped(idx):
    return np.tile(np.asarray(idx).reshape(-1, 16).T, (8, 1)).astype(np.uint16)


def unstriped(offs):
    return offs[:16].T.reshape(-1).astype(np.int64)


def striped8(idx):
    return np.asarray(idx).reshape(8, -1, 16).transpose(0, 2, 1).reshape(128, -1).astype(np.uint16)


def unstriped8(offs):
    return offs.reshape(8, 16, -1).transpose(0, 2, 1).reshape(8, -1).astype(np.int64)


def pick8(x, idx, run):
    r = np.arange(len(x))
    return x[r[:, None], idx[r % (8 * run) // run]]


E2M1 = np.array([0.0, 0.5, 1.0, 1.5, 2.0, 3.0, 4.0, 6.0, -0.0, -0.5, -1.0, -1.5, -2.0, -3.0, -4.0, -6.0])


def pack_weight(w, fmt):
    k, n = w.shape
    w = f64(np.asarray(w, np.float32).astype(ml_dtypes.bfloat16)).reshape(k // 32, 32, n)
    amax = np.abs(w).max(1)
    if fmt in ("e4m3", "e5m2"):
        byte = np.frexp(amax)[1] - 1 + 127 - (7 if fmt == "e4m3" else 14)
    else:
        mant, ex = np.frexp(amax / 6.0)
        byte = np.where(mant > 0.5, ex, ex - 1) + 127
    byte = np.clip(np.where(amax > 0, byte, 1), 1, 254)
    scaled = (w * np.exp2(127.0 - byte)[:, None, :]).reshape(k, n).astype(np.float32)
    by_word = np.ascontiguousarray(scaled.reshape(k // 512, 128, 4, n).transpose(0, 1, 3, 2))
    if fmt in ("e4m3", "e5m2"):
        words = by_word.astype(ml_dtypes.float8_e4m3fn if fmt == "e4m3" else ml_dtypes.float8_e5m2).view(np.uint8)
    else:
        c = by_word.astype(ml_dtypes.float4_e2m1fn).view(np.uint8) & 0xF
        words = (c[..., 0::2] | (c[..., 1::2] << 4)).reshape(k // 512, 128, 2 * n)
    return np.ascontiguousarray(words), np.ascontiguousarray(byte.astype(np.uint8).reshape(k // 512, 16, n))


def unpack_weight(words, scales, fmt):
    g, _, n = scales.shape
    words = np.ascontiguousarray(words).reshape(g, 128, n, -1)
    if fmt in ("e4m3", "e5m2"):
        vals = words.view(ml_dtypes.float8_e4m3fn if fmt == "e4m3" else ml_dtypes.float8_e5m2).astype(np.float64)
    else:
        nib = np.empty((g, 128, n, 4), np.uint8)
        nib[..., 0::2] = words & 0xF
        nib[..., 1::2] = words >> 4
        vals = E2M1[nib]
    vals = vals * np.repeat(np.exp2(scales.astype(np.float64) - 127.0), 8, axis=1)[..., None]
    return vals.transpose(0, 1, 3, 2).reshape(g * 512, n)


K, T, J, R, O, N = 512, 512, 256, 512, 128, 256


def setup_inputs():
    n = np.random.standard_normal
    idx = np.stack([np.random.permutation(T)[:J] for _ in range(8)])
    idx2 = np.random.permutation(J)[:O]
    idx3 = np.random.permutation(J)[:O]
    fk = mx_kscale(K)
    fr = mx_kscale(R)
    xtp = pack_weight(n((K, T)) / fk[:, None], "e4m3")
    wp = pack_weight(n((K, R)) * 1 / np.sqrt(K) * fk[:, None] * fr, "e2m1")
    wbp = pack_weight(n((R, N)) * np.random.uniform(0.3, 1.7, (1, N)) / np.sqrt(R) / fr[:, None], "e5m2")
    return {
        "xt_words": xtp[0],
        "xt_scales": xtp[1],
        "w_words": wp[0],
        "w_scales": wp[1],
        "wb_words": wbp[0],
        "wb_scales": wbp[1],
        "rs": (0.6 * n((N, O)) * np.random.uniform(0.2, 2.5, (N, 1)) + np.random.uniform(-1.0, 1.0, (N, 1))).astype(np.float32),
        "offs": striped8(idx),
        "offs2": striped(idx2),
        "offs3": striped(idx3),
    }


def reference(xt_words, xt_scales, w_words, w_scales, wb_words, wb_scales, rs, offs, offs2, offs3):
    idx = unstriped8(offs)
    idx2 = unstriped(offs2)
    idx3 = unstriped(offs3)
    xtu = unpack_weight(xt_words, xt_scales, "e4m3")
    wu = unpack_weight(w_words, w_scales, "e2m1")
    wbu = unpack_weight(wb_words, wb_scales, "e5m2")
    xtidxg = pick8(xtu, idx, 64)
    a = wu.T @ xtidxg
    hid = np.abs(a[:, idx2] - 0.5 * a[:, idx3])
    hidq = mxq(hid, 0, "e5m2")
    p = wbu.T @ hidq
    pb = p + f64(rs)
    mn = np.mean(pb, axis=1, keepdims=True)
    d = pb - mn
    y = d / np.sqrt(np.mean(np.square(d), axis=1, keepdims=True) + 0.1)
    return y

@@ -1,0 +1,154 @@
+from contextlib import ExitStack
+
+import concourse.mybir as mybir
+
+K, T, J, R, O, N = 512, 512, 256, 512, 128, 256
+FLOPS = 2 * K * R * J + 2 * R * N * O
+
+F32 = mybir.dt.float32
+BF16 = mybir.dt.bfloat16
+I32 = mybir.dt.int32
+U32 = mybir.dt.uint32
+U16 = mybir.dt.uint16
+U8 = mybir.dt.uint8
+E4M3X4 = mybir.dt.float8_e4m3fn_x4
+E5M2X4 = mybir.dt.float8_e5m2_x4
+E2M1X4 = mybir.dt.float4_e2m1fn_x4
+ALU = mybir.AluOpType
+ACT = mybir.ActivationFunctionType
+
+P = 128
+PACK = 4
+QUAD = 32
+EPS = 0.1
+
+
+def tile_list_looks_headpicks_farther_levelled_kernel(
+    tc, xt_words, xt_scales, w_words, w_scales, wb_words, wb_scales, rs, offs, offs2, offs3, out
+):
+    nc = tc.nc
+    with ExitStack() as ctx:
+        sb = ctx.enter_context(tc.tile_pool(name="sb", bufs=1))
+        ps = ctx.enter_context(tc.psum_pool(name="ps", bufs=1))
+
+        lists = sb.tile([P, J // 16], U16, name="lists")
+        list2 = sb.tile([P, O // 16], U16, name="list2")
+        list3 = sb.tile([P, O // 16], U16, name="list3")
+        x_bytes = sb.tile([P, T], U8, name="x_bytes", align_bytes=64)
+        x_words = sb.tile([P, T], I32, name="x_words", align_bytes=64)
+        raw_words = sb.tile([P, 2 * R], U8, name="raw_words", align_bytes=64)
+        raw_bytes = sb.tile([P, R], U8, name="raw_bytes", align_bytes=64)
+        xg_bytes = sb.tile([P, J], U8, name="xg_bytes", align_bytes=64)
+        xg_words = sb.tile([P, J], U32, name="xg_words", align_bytes=64)
+        xg_plane = sb.tile([P, J], U8, name="xg_plane", align_bytes=64)
+        w_dealt = sb.tile([P, 2 * R], U8, name="w_dealt", align_bytes=64)
+        w_plane = sb.tile([P, R], U8, name="w_plane", align_bytes=64)
+        resid = sb.tile([P, N // P, O], F32, name="resid")
+
+        nc.vector.memset(x_bytes[:].bitcast(I32), 0)
+        nc.vector.memset(raw_bytes[:].bitcast(I32), 0)
+        nc.vector.memset(xg_plane[:].bitcast(I32), 0)
+
+        nc.sync.dma_start(lists[:], offs)
+        nc.sync.dma_start(x_bytes[0:P:8, :].bitcast(I32), xt_scales[0].bitcast(I32))
+        nc.sync.dma_start(x_words[:], xt_words[0].rearrange("p n t -> p (n t)").bitcast(I32))
+        nc.sync.dma_start(raw_words[:].bitcast(I32), w_words[0].bitcast(I32))
+        for x in range(4):
+            nc.scalar.dma_start(
+                raw_bytes[QUAD * x : QUAD * x + 4, :].bitcast(I32), w_scales[0, 4 * x : 4 * x + 4, :].bitcast(I32)
+            )
+        nc.sync.dma_start(list3[:], offs3)
+        nc.sync.dma_start(list2[:], offs2)
+        nc.scalar.dma_start(resid[:], rs.rearrange("(c p) o -> p c o", p=P))
+
+        nc.vector.tensor_copy(xg_bytes[:], x_bytes[:].indirect(lists[:]))
+        for x in range(4):
+            queue = nc.sync if x % 2 == 0 else nc.scalar
+            queue.dma_start(
+                xg_plane[QUAD * x : QUAD * x + 4, :].bitcast(I32),
+                xg_bytes[QUAD * x : QUAD * (x + 1) : 8, :].bitcast(I32),
+            )
+        nc.vector.tensor_copy(xg_words[:], x_words[:].bitcast(U32).indirect(lists[:]))
+        nc.vector.tensor_copy(
+            w_plane[:].rearrange("p (t m) -> p t m", t=PACK), raw_bytes[:].rearrange("p (m t) -> p t m", t=PACK)
+        )
+        nc.vector.tensor_copy(
+            w_dealt[:].bitcast(U16).rearrange("p (t m) -> p t m", t=PACK),
+            raw_words[:].bitcast(U16).rearrange("p (m t) -> p t m", t=PACK),
+        )
+
+        for x in range(4):
+            nc.sync.dma_start(
+                raw_bytes[QUAD * x : QUAD * x + 4, 0:N].bitcast(I32), wb_scales[0, 4 * x : 4 * x + 4, :].bitcast(I32)
+            )
+        nc.sync.dma_start(raw_words[:].bitcast(I32), wb_words[0].rearrange("p n t -> p (n t)").bitcast(I32))
+
+        diff = sb.tile([P, PACK, O], F32, name="diff")
+        a_sb = []
+        for t in range(PACK):
+            acc = ps.tile([P, J], F32, name="acc%d" % t)
+            nc.tensor.matmul_mx(
+                out=acc[:],
+                lhsT=w_dealt[:, 2 * P * t : 2 * P * (t + 1)].bitcast(E2M1X4),
+                lhsT_scale=w_plane[:, P * t : P * (t + 1)],
+                rhs=xg_words[:].bitcast(E4M3X4),
+                rhs_scale=xg_plane[:],
+                start=True,
+                stop=True,
+            )
+            a_t = sb.tile([P, J], F32, name="a%d" % t)
+            if t % 2 == 0:
+                nc.scalar.copy(a_t[:], acc[:])
+            else:
+                nc.vector.tensor_copy(a_t[:], acc[:])
+            a_sb.append(a_t)
+        for t in range(PACK):
+            half = sb.tile([P, O], F32, name="half%d" % t)
+            nc.scalar.activation(half[:], a_sb[t][:].indirect(list3[:]), ACT.Copy, scale=-0.5)
+            nc.vector.tensor_tensor(diff[:, t, :], a_sb[t][:].indirect(list2[:]), half[:], ALU.add)
+
+        hid = sb.tile([P, O, PACK], BF16, name="hid", align_bytes=64)
+        woven = diff[:].rearrange("p t o -> p o t")
+        H = O // 2
+        nc.scalar.activation(hid[:, 0:H, :], woven[:, 0:H, :], ACT.Abs)
+        nc.vector.scalar_tensor_tensor(hid[:, H:O, :], woven[:, H:O, :], -1.0, woven[:, H:O, :], ALU.mult, ALU.max)
+        h_words = sb.tile([P, O], U32, name="h_words", align_bytes=64)
+        h_plane = sb.tile([P, O], U8, name="h_plane", align_bytes=64)
+        nc.vector.quantize_mx(
+            out=h_words[:].bitcast(E5M2X4), scales=h_plane[:], in_=hid[:].rearrange("p o t -> p (o t)")
+        )
+
+        total = sb.tile([P, N // P], F32, name="total")
+        sumsq = sb.tile([P, N // P], F32, name="sumsq")
+        inv = sb.tile([P, N // P], F32, name="inv")
+        wb_codes = raw_words[:].bitcast(U32)
+        centred = []
+        for c in range(N // P):
+            acc = ps.tile([P, O], F32, name="p%d" % c)
+            nc.tensor.matmul_mx(
+                out=acc[:],
+                lhsT=wb_codes[:, P * c : P * (c + 1)].bitcast(E5M2X4),
+                lhsT_scale=raw_bytes[:, P * c : P * (c + 1)],
+                rhs=h_words[:].bitcast(E5M2X4),
+                rhs_scale=h_plane[:],
+                start=True,
+                stop=True,
+            )
+            pb = sb.tile([P, O], F32, name="pb%d" % c)
+            nc.vector.scalar_tensor_tensor(
+                pb[:], acc[:], 1.0, resid[:, c, :], ALU.mult, ALU.add, accum_out=total[:, c : c + 1]
+            )
+            squares = sb.tile([P, O], F32, name="squares%d" % c)
+            nc.scalar.activation(
+                squares[:], pb[:], ACT.Square, bias=total[:, c : c + 1], scale=-float(O), accum_out=sumsq[:, c : c + 1]
+            )
+            d_c = sb.tile([P, O], F32, name="d%d" % c)
+            nc.vector.tensor_scalar(d_c[:], pb[:], float(O), total[:, c : c + 1], ALU.mult, ALU.subtract)
+            centred.append(d_c)
+        nc.scalar.activation(inv[:], sumsq[:], ACT.Abs_reciprocal_sqrt, bias=EPS * O * O, scale=1.0 / O)
+        y0 = sb.tile([P, O], F32, name="y0")
+        y1 = sb.tile([P, O], F32, name="y1")
+        nc.scalar.activation(y0[:], centred[0][:], ACT.Copy, scale=inv[:, 0:1])
+        nc.vector.tensor_scalar(y1[:], centred[1][:], inv[:, 1:2], None, ALU.mult)
+        nc.scalar.dma_start(out[0:P, :], y0[:])
+        nc.sync.dma_start(out[P : 2 * P, :], y1[:])

@@ -35,7 +35,7 @@ def tile_list_looks_headpicks_farther_levelled_kernel(
         list2 = sb.tile([P, O // 16], U16, name="list2")
         list3 = sb.tile([P, O // 16], U16, name="list3")
         x_bytes = sb.tile([P, T], U8, name="x_bytes", align_bytes=64)
-        x_words = sb.tile([P, T], I32, name="x_words", align_bytes=64)
+        x_words = sb.tile([P, T], I32, name="x_words", tag="early_then_late", align_bytes=64)
         raw_words = sb.tile([P, 2 * R], U8, name="raw_words", align_bytes=64)
         raw_bytes = sb.tile([P, R], U8, name="raw_bytes", align_bytes=64)
         xg_bytes = sb.tile([P, J], U8, name="xg_bytes", align_bytes=64)
@@ -43,23 +43,25 @@ def tile_list_looks_headpicks_farther_levelled_kernel(
         xg_plane = sb.tile([P, J], U8, name="xg_plane", align_bytes=64)
         w_dealt = sb.tile([P, 2 * R], U8, name="w_dealt", align_bytes=64)
         w_plane = sb.tile([P, R], U8, name="w_plane", align_bytes=64)
-        resid = sb.tile([P, N // P, O], F32, name="resid")
+        warm = sb.tile([P, 2], F32, name="warm")
 
-        nc.vector.memset(x_bytes[:].bitcast(I32), 0)
         nc.vector.memset(raw_bytes[:].bitcast(I32), 0)
+        nc.vector.memset(warm[:, 0:1], 1.0)
         nc.vector.memset(xg_plane[:].bitcast(I32), 0)
 
         nc.sync.dma_start(lists[:], offs)
-        nc.sync.dma_start(x_bytes[0:P:8, :].bitcast(I32), xt_scales[0].bitcast(I32))
-        nc.sync.dma_start(x_words[:], xt_words[0].rearrange("p n t -> p (n t)").bitcast(I32))
-        nc.sync.dma_start(raw_words[:].bitcast(I32), w_words[0].bitcast(I32))
-        for x in range(4):
-            nc.scalar.dma_start(
-                raw_bytes[QUAD * x : QUAD * x + 4, :].bitcast(I32), w_scales[0, 4 * x : 4 * x + 4, :].bitcast(I32)
-            )
+        nc.scalar.dma_start(
+            x_bytes[:].bitcast(I32), xt_scales[0].bitcast(I32).unsqueeze(1).to_broadcast([16, 8, T // 4])
+        )
         nc.sync.dma_start(list3[:], offs3)
         nc.sync.dma_start(list2[:], offs2)
-        nc.scalar.dma_start(resid[:], rs.rearrange("(c p) o -> p c o", p=P))
+        nc.sync.dma_start(raw_words[:].bitcast(I32), w_words[0].bitcast(I32))
+        nc.sync.dma_start(x_words[:], xt_words[0].rearrange("p n t -> p (n t)").bitcast(I32))
+        for x in range(4):
+            nc.sync.dma_start(
+                raw_bytes[QUAD * x : QUAD * x + 4, :].bitcast(I32), w_scales[0, 4 * x : 4 * x + 4, :].bitcast(I32)
+            )
+        nc.scalar.activation(warm[:, 1:2], warm[:, 0:1], ACT.Abs_reciprocal_sqrt)
 
         nc.vector.tensor_copy(xg_bytes[:], x_bytes[:].indirect(lists[:]))
         for x in range(4):
@@ -82,6 +84,9 @@ def tile_list_looks_headpicks_farther_levelled_kernel(
                 raw_bytes[QUAD * x : QUAD * x + 4, 0:N].bitcast(I32), wb_scales[0, 4 * x : 4 * x + 4, :].bitcast(I32)
             )
         nc.sync.dma_start(raw_words[:].bitcast(I32), wb_words[0].rearrange("p n t -> p (n t)").bitcast(I32))
+
+        resid = sb.tile([P, N // P, O], F32, name="resid", tag="early_then_late", align_bytes=64)
+        nc.sync.dma_start(resid[:], rs.rearrange("(c p) o -> p c o", p=P))
 
         diff = sb.tile([P, PACK, O], F32, name="diff")
         a_sb = []
@@ -110,8 +115,11 @@ def tile_list_looks_headpicks_farther_levelled_kernel(
         hid = sb.tile([P, O, PACK], BF16, name="hid", align_bytes=64)
         woven = diff[:].rearrange("p t o -> p o t")
         H = O // 2
-        nc.scalar.activation(hid[:, 0:H, :], woven[:, 0:H, :], ACT.Abs)
-        nc.vector.scalar_tensor_tensor(hid[:, H:O, :], woven[:, H:O, :], -1.0, woven[:, H:O, :], ALU.mult, ALU.max)
+        nc.scalar.activation(hid[:, :, 0:2], woven[:, :, 0:2], ACT.Abs)
+        nc.scalar.activation(hid[:, 0:H, 2:4], woven[:, 0:H, 2:4], ACT.Abs)
+        nc.vector.scalar_tensor_tensor(
+            hid[:, H:O, 2:4], woven[:, H:O, 2:4], -1.0, woven[:, H:O, 2:4], ALU.mult, ALU.max
+        )
         h_words = sb.tile([P, O], U32, name="h_words", align_bytes=64)
         h_plane = sb.tile([P, O], U8, name="h_plane", align_bytes=64)
         nc.vector.quantize_mx(
@@ -123,6 +131,7 @@ def tile_list_looks_headpicks_farther_levelled_kernel(
         inv = sb.tile([P, N // P], F32, name="inv")
         wb_codes = raw_words[:].bitcast(U32)
         centred = []
+        sums = []
         for c in range(N // P):
             acc = ps.tile([P, O], F32, name="p%d" % c)
             nc.tensor.matmul_mx(
@@ -138,6 +147,8 @@ def tile_list_looks_headpicks_farther_levelled_kernel(
             nc.vector.scalar_tensor_tensor(
                 pb[:], acc[:], 1.0, resid[:, c, :], ALU.mult, ALU.add, accum_out=total[:, c : c + 1]
             )
+            sums.append(pb)
+        for c, pb in enumerate(sums):
             squares = sb.tile([P, O], F32, name="squares%d" % c)
             nc.scalar.activation(
                 squares[:], pb[:], ACT.Square, bias=total[:, c : c + 1], scale=-float(O), accum_out=sumsq[:, c : c + 1]

@@ -88,37 +88,39 @@ def tile_list_looks_headpicks_farther_levelled_kernel(
         resid = sb.tile([P, N // P, O], F32, name="resid", tag="early_then_late", align_bytes=64)
         nc.sync.dma_start(resid[:], rs.rearrange("(c p) o -> p c o", p=P))
 
-        diff = sb.tile([P, PACK, O], F32, name="diff")
+        diff = [sb.tile([P, 2, O], F32, name="diff%d" % u) for u in range(2)]
         a_sb = []
+        plan = ["sv", "v", "v", "v"]
         for t in range(PACK):
-            acc = ps.tile([P, J], F32, name="acc%d" % t)
-            nc.tensor.matmul_mx(
-                out=acc[:],
-                lhsT=w_dealt[:, 2 * P * t : 2 * P * (t + 1)].bitcast(E2M1X4),
-                lhsT_scale=w_plane[:, P * t : P * (t + 1)],
-                rhs=xg_words[:].bitcast(E4M3X4),
-                rhs_scale=xg_plane[:],
-                start=True,
-                stop=True,
-            )
             a_t = sb.tile([P, J], F32, name="a%d" % t)
-            if t % 2 == 0:
-                nc.scalar.copy(a_t[:], acc[:])
-            else:
-                nc.vector.tensor_copy(a_t[:], acc[:])
-            a_sb.append(a_t)
-        for t in range(PACK):
+            width = J // len(plan[t])
+            for i, engine in enumerate(plan[t]):
+                cols = slice(i * width, (i + 1) * width)
+                acc = ps.tile([P, width], F32, name="acc%d_%d" % (t, i))
+                nc.tensor.matmul_mx(
+                    out=acc[:],
+                    lhsT=w_dealt[:, 2 * P * t : 2 * P * (t + 1)].bitcast(E2M1X4),
+                    lhsT_scale=w_plane[:, P * t : P * (t + 1)],
+                    rhs=xg_words[:, cols].bitcast(E4M3X4),
+                    rhs_scale=xg_plane[:, cols],
+                    start=True,
+                    stop=True,
+                )
+                if engine == "s":
+                    nc.scalar.copy(a_t[:, cols], acc[:])
+                else:
+                    nc.vector.tensor_copy(a_t[:, cols], acc[:])
             half = sb.tile([P, O], F32, name="half%d" % t)
-            nc.scalar.activation(half[:], a_sb[t][:].indirect(list3[:]), ACT.Copy, scale=-0.5)
-            nc.vector.tensor_tensor(diff[:, t, :], a_sb[t][:].indirect(list2[:]), half[:], ALU.add)
+            nc.scalar.activation(half[:], a_t[:].indirect(list3[:]), ACT.Copy, scale=-0.5)
+            nc.vector.tensor_tensor(diff[t // 2][:, t % 2, :], a_t[:].indirect(list2[:]), half[:], ALU.add)
 
         hid = sb.tile([P, O, PACK], BF16, name="hid", align_bytes=64)
-        woven = diff[:].rearrange("p t o -> p o t")
+        woven = [pair[:].rearrange("p t o -> p o t") for pair in diff]
         H = O // 2
-        nc.scalar.activation(hid[:, :, 0:2], woven[:, :, 0:2], ACT.Abs)
-        nc.scalar.activation(hid[:, 0:H, 2:4], woven[:, 0:H, 2:4], ACT.Abs)
+        nc.scalar.activation(hid[:, :, 0:2], woven[0], ACT.Abs)
+        nc.scalar.activation(hid[:, 0:H, 2:4], woven[1][:, 0:H, :], ACT.Abs)
         nc.vector.scalar_tensor_tensor(
-            hid[:, H:O, 2:4], woven[:, H:O, 2:4], -1.0, woven[:, H:O, 2:4], ALU.mult, ALU.max
+            hid[:, H:O, 2:4], woven[1][:, H:O, :], -1.0, woven[1][:, H:O, :], ALU.mult, ALU.max
         )
         h_words = sb.tile([P, O], U32, name="h_words", align_bytes=64)
         h_plane = sb.tile([P, O], U8, name="h_plane", align_bytes=64)

@@ -45,7 +45,6 @@ def tile_list_looks_headpicks_farther_levelled_kernel(
         w_plane = sb.tile([P, R], U8, name="w_plane", align_bytes=64)
         warm = sb.tile([P, 2], F32, name="warm")
 
-        nc.vector.memset(raw_bytes[:].bitcast(I32), 0)
         nc.vector.memset(warm[:, 0:1], 1.0)
         nc.vector.memset(xg_plane[:].bitcast(I32), 0)
 
@@ -55,12 +54,18 @@ def tile_list_looks_headpicks_farther_levelled_kernel(
         )
         nc.sync.dma_start(list3[:], offs3)
         nc.sync.dma_start(list2[:], offs2)
+        def load_w_scales(x):
+            rows = w_scales[0, 4 * x : 4 * x + 4, :].bitcast(I32)
+            nc.sync.dma_start(
+                raw_bytes[QUAD * x : QUAD * (x + 1), :].bitcast(I32), rows.unsqueeze(0).to_broadcast([8, 4, R // 4])
+            )
+
+        load_w_scales(0)
         nc.sync.dma_start(raw_words[:].bitcast(I32), w_words[0].bitcast(I32))
         nc.sync.dma_start(x_words[:], xt_words[0].rearrange("p n t -> p (n t)").bitcast(I32))
-        for x in range(4):
-            nc.sync.dma_start(
-                raw_bytes[QUAD * x : QUAD * x + 4, :].bitcast(I32), w_scales[0, 4 * x : 4 * x + 4, :].bitcast(I32)
-            )
+        load_w_scales(1)
+        load_w_scales(2)
+        load_w_scales(3)
         nc.scalar.activation(warm[:, 1:2], warm[:, 0:1], ACT.Abs_reciprocal_sqrt)
 
         nc.vector.tensor_copy(xg_bytes[:], x_bytes[:].indirect(lists[:]))
@@ -70,13 +75,13 @@ def tile_list_looks_headpicks_farther_levelled_kernel(
                 xg_plane[QUAD * x : QUAD * x + 4, :].bitcast(I32),
                 xg_bytes[QUAD * x : QUAD * (x + 1) : 8, :].bitcast(I32),
             )
-        nc.vector.tensor_copy(xg_words[:], x_words[:].bitcast(U32).indirect(lists[:]))
-        nc.vector.tensor_copy(
-            w_plane[:].rearrange("p (t m) -> p t m", t=PACK), raw_bytes[:].rearrange("p (m t) -> p t m", t=PACK)
-        )
         nc.vector.tensor_copy(
             w_dealt[:].bitcast(U16).rearrange("p (t m) -> p t m", t=PACK),
             raw_words[:].bitcast(U16).rearrange("p (m t) -> p t m", t=PACK),
+        )
+        nc.vector.tensor_copy(xg_words[:], x_words[:].bitcast(U32).indirect(lists[:]))
+        nc.vector.tensor_copy(
+            w_plane[:].rearrange("p (t m) -> p t m", t=PACK), raw_bytes[:].rearrange("p (m t) -> p t m", t=PACK)
         )
 
         for x in range(4):
@@ -158,10 +163,11 @@ def tile_list_looks_headpicks_farther_levelled_kernel(
             d_c = sb.tile([P, O], F32, name="d%d" % c)
             nc.vector.tensor_scalar(d_c[:], pb[:], float(O), total[:, c : c + 1], ALU.mult, ALU.subtract)
             centred.append(d_c)
-        nc.scalar.activation(inv[:], sumsq[:], ACT.Abs_reciprocal_sqrt, bias=EPS * O * O, scale=1.0 / O)
-        y0 = sb.tile([P, O], F32, name="y0")
-        y1 = sb.tile([P, O], F32, name="y1")
-        nc.scalar.activation(y0[:], centred[0][:], ACT.Copy, scale=inv[:, 0:1])
-        nc.vector.tensor_scalar(y1[:], centred[1][:], inv[:, 1:2], None, ALU.mult)
-        nc.scalar.dma_start(out[0:P, :], y0[:])
-        nc.sync.dma_start(out[P : 2 * P, :], y1[:])
+        for c, d_c in enumerate(centred):
+            nc.scalar.activation(
+                inv[:, c : c + 1], sumsq[:, c : c + 1], ACT.Abs_reciprocal_sqrt, bias=EPS * O * O, scale=1.0 / O
+            )
+            y = sb.tile([P, O], F32, name="y%d" % c)
+            nc.vector.tensor_scalar(y[:], d_c[:], inv[:, c : c + 1], None, ALU.mult)
+            queue = nc.scalar if c == 0 else nc.sync
+            queue.dma_start(out[P * c : P * (c + 1), :], y[:])

from contextlib import ExitStack

import concourse.mybir as mybir

K, T, J, R, O, N = 512, 512, 256, 512, 128, 256
FLOPS = 2 * K * R * J + 2 * R * N * O

F32 = mybir.dt.float32
BF16 = mybir.dt.bfloat16
I32 = mybir.dt.int32
U32 = mybir.dt.uint32
U16 = mybir.dt.uint16
U8 = mybir.dt.uint8
E4M3X4 = mybir.dt.float8_e4m3fn_x4
E5M2X4 = mybir.dt.float8_e5m2_x4
E2M1X4 = mybir.dt.float4_e2m1fn_x4
ALU = mybir.AluOpType
ACT = mybir.ActivationFunctionType

P = 128
PACK = 4
QUAD = 32
EPS = 0.1


def tile_list_looks_headpicks_farther_levelled_kernel(
    tc, xt_words, xt_scales, w_words, w_scales, wb_words, wb_scales, rs, offs, offs2, offs3, out
):
    nc = tc.nc
    with ExitStack() as ctx:
        sb = ctx.enter_context(tc.tile_pool(name="sb", bufs=1))
        ps = ctx.enter_context(tc.psum_pool(name="ps", bufs=1))

        lists = sb.tile([P, J // 16], U16, name="lists")
        list2 = sb.tile([P, O // 16], U16, name="list2")
        list3 = sb.tile([P, O // 16], U16, name="list3")
        x_bytes = sb.tile([P, T], U8, name="x_bytes", align_bytes=64)
        x_words = sb.tile([P, T], I32, name="x_words", tag="early_then_late", align_bytes=64)
        raw_words = sb.tile([P, 2 * R], U8, name="raw_words", align_bytes=64)
        raw_bytes = sb.tile([P, R], U8, name="raw_bytes", align_bytes=64)
        xg_bytes = sb.tile([P, J], U8, name="xg_bytes", align_bytes=64)
        xg_words = sb.tile([P, J], U32, name="xg_words", align_bytes=64)
        xg_plane = sb.tile([P, J], U8, name="xg_plane", align_bytes=64)
        w_dealt = sb.tile([P, 2 * R], U8, name="w_dealt", align_bytes=64)
        w_plane = sb.tile([P, R], U8, name="w_plane", align_bytes=64)
        warm = sb.tile([P, 2], F32, name="warm")

        nc.vector.memset(warm[:, 0:1], 1.0)
        nc.vector.memset(xg_plane[:].bitcast(I32), 0)

        nc.sync.dma_start(lists[:], offs)
        nc.scalar.dma_start(
            x_bytes[:].bitcast(I32), xt_scales[0].bitcast(I32).unsqueeze(1).to_broadcast([16, 8, T // 4])
        )
        nc.sync.dma_start(list3[:], offs3)
        nc.sync.dma_start(list2[:], offs2)
        def load_w_scales(x):
            rows = w_scales[0, 4 * x : 4 * x + 4, :].bitcast(I32)
            nc.sync.dma_start(
                raw_bytes[QUAD * x : QUAD * (x + 1), :].bitcast(I32), rows.unsqueeze(0).to_broadcast([8, 4, R // 4])
            )

        load_w_scales(0)
        nc.sync.dma_start(raw_words[:].bitcast(I32), w_words[0].bitcast(I32))
        nc.sync.dma_start(x_words[:], xt_words[0].rearrange("p n t -> p (n t)").bitcast(I32))
        load_w_scales(1)
        load_w_scales(2)
        load_w_scales(3)
        nc.scalar.activation(warm[:, 1:2], warm[:, 0:1], ACT.Abs_reciprocal_sqrt)

        nc.vector.tensor_copy(xg_bytes[:], x_bytes[:].indirect(lists[:]))
        for x in range(4):
            queue = nc.sync if x % 2 == 0 else nc.scalar
            queue.dma_start(
                xg_plane[QUAD * x : QUAD * x + 4, :].bitcast(I32),
                xg_bytes[QUAD * x : QUAD * (x + 1) : 8, :].bitcast(I32),
            )
        nc.vector.tensor_copy(
            w_dealt[:].bitcast(U16).rearrange("p (t m) -> p t m", t=PACK),
            raw_words[:].bitcast(U16).rearrange("p (m t) -> p t m", t=PACK),
        )
        nc.vector.tensor_copy(xg_words[:], x_words[:].bitcast(U32).indirect(lists[:]))
        nc.vector.tensor_copy(
            w_plane[:].rearrange("p (t m) -> p t m", t=PACK), raw_bytes[:].rearrange("p (m t) -> p t m", t=PACK)
        )

        for x in range(4):
            nc.sync.dma_start(
                raw_bytes[QUAD * x : QUAD * x + 4, 0:N].bitcast(I32), wb_scales[0, 4 * x : 4 * x + 4, :].bitcast(I32)
            )
        nc.sync.dma_start(raw_words[:].bitcast(I32), wb_words[0].rearrange("p n t -> p (n t)").bitcast(I32))

        resid = sb.tile([P, N // P, O], F32, name="resid", tag="early_then_late", align_bytes=64)
        nc.sync.dma_start(resid[:], rs.rearrange("(c p) o -> p c o", p=P))

        diff = [sb.tile([P, 2, O], F32, name="diff%d" % u) for u in range(2)]
        a_sb = []
        plan = ["sv", "v", "v", "v"]
        for t in range(PACK):
            a_t = sb.tile([P, J], F32, name="a%d" % t)
            width = J // len(plan[t])
            for i, engine in enumerate(plan[t]):
                cols = slice(i * width, (i + 1) * width)
                acc = ps.tile([P, width], F32, name="acc%d_%d" % (t, i))
                nc.tensor.matmul_mx(
                    out=acc[:],
                    lhsT=w_dealt[:, 2 * P * t : 2 * P * (t + 1)].bitcast(E2M1X4),
                    lhsT_scale=w_plane[:, P * t : P * (t + 1)],
                    rhs=xg_words[:, cols].bitcast(E4M3X4),
                    rhs_scale=xg_plane[:, cols],
                    start=True,
                    stop=True,
                )
                if engine == "s":
                    nc.scalar.copy(a_t[:, cols], acc[:])
                else:
                    nc.vector.tensor_copy(a_t[:, cols], acc[:])
            half = sb.tile([P, O], F32, name="half%d" % t)
            nc.scalar.activation(half[:], a_t[:].indirect(list3[:]), ACT.Copy, scale=-0.5)
            nc.vector.tensor_tensor(diff[t // 2][:, t % 2, :], a_t[:].indirect(list2[:]), half[:], ALU.add)

        hid = sb.tile([P, O, PACK], BF16, name="hid", align_bytes=64)
        woven = [pair[:].rearrange("p t o -> p o t") for pair in diff]
        H = O // 2
        nc.scalar.activation(hid[:, :, 0:2], woven[0], ACT.Abs)
        nc.scalar.activation(hid[:, 0:H, 2:4], woven[1][:, 0:H, :], ACT.Abs)
        nc.vector.scalar_tensor_tensor(
            hid[:, H:O, 2:4], woven[1][:, H:O, :], -1.0, woven[1][:, H:O, :], ALU.mult, ALU.max
        )
        h_words = sb.tile([P, O], U32, name="h_words", align_bytes=64)
        h_plane = sb.tile([P, O], U8, name="h_plane", align_bytes=64)
        nc.vector.quantize_mx(
            out=h_words[:].bitcast(E5M2X4), scales=h_plane[:], in_=hid[:].rearrange("p o t -> p (o t)")
        )

        total = sb.tile([P, N // P], F32, name="total")
        sumsq = sb.tile([P, N // P], F32, name="sumsq")
        inv = sb.tile([P, N // P], F32, name="inv")
        wb_codes = raw_words[:].bitcast(U32)
        centred = []
        sums = []
        for c in range(N // P):
            acc = ps.tile([P, O], F32, name="p%d" % c)
            nc.tensor.matmul_mx(
                out=acc[:],
                lhsT=wb_codes[:, P * c : P * (c + 1)].bitcast(E5M2X4),
                lhsT_scale=raw_bytes[:, P * c : P * (c + 1)],
                rhs=h_words[:].bitcast(E5M2X4),
                rhs_scale=h_plane[:],
                start=True,
                stop=True,
            )
            pb = sb.tile([P, O], F32, name="pb%d" % c)
            nc.vector.scalar_tensor_tensor(
                pb[:], acc[:], 1.0, resid[:, c, :], ALU.mult, ALU.add, accum_out=total[:, c : c + 1]
            )
            sums.append(pb)
        for c, pb in enumerate(sums):
            squares = sb.tile([P, O], F32, name="squares%d" % c)
            nc.scalar.activation(
                squares[:], pb[:], ACT.Square, bias=total[:, c : c + 1], scale=-float(O), accum_out=sumsq[:, c : c + 1]
            )
            d_c = sb.tile([P, O], F32, name="d%d" % c)
            nc.vector.tensor_scalar(d_c[:], pb[:], float(O), total[:, c : c + 1], ALU.mult, ALU.subtract)
            centred.append(d_c)
        for c, d_c in enumerate(centred):
            nc.scalar.activation(
                inv[:, c : c + 1], sumsq[:, c : c + 1], ACT.Abs_reciprocal_sqrt, bias=EPS * O * O, scale=1.0 / O
            )
            y = sb.tile([P, O], F32, name="y%d" % c)
            nc.vector.tensor_scalar(y[:], d_c[:], inv[:, c : c + 1], None, ALU.mult)
            queue = nc.scalar if c == 0 else nc.sync
            queue.dma_start(out[P * c : P * (c + 1), :], y[:])
